import numpy as np
import ml_dtypes


def mxq(x, axis, fmt="e4m3"):
    dtype, down = {"e4m3": (ml_dtypes.float8_e4m3fn, 7), "e5m2": (ml_dtypes.float8_e5m2, 14)}[fmt]
    v = np.moveaxis(np.asarray(x, np.float32).astype(ml_dtypes.bfloat16).astype(np.float64), axis, -1)
    blocks = v.reshape(v.shape[:-1] + (-1, 32))
    amax = np.abs(blocks).max(-1, keepdims=True)
    byte = np.maximum(np.where(amax > 0, np.frexp(amax)[1] - 1 + 127, 0) - down, 1)
    scale = np.exp2(byte - 127.0)
    codes = (blocks / scale).astype(np.float32).astype(dtype).astype(np.float64)
    return np.moveaxis((codes * scale).reshape(v.shape), -1, axis)


WIDE = False


def mx_kscale(k, group=512):
    if not WIDE:
        return np.ones(k)
    levels = np.array([18, -18])
    if group != 512:
        return np.exp2(np.random.permutation(np.resize(levels, k // group))).repeat(group)
    if k % 512:
        return np.exp2(np.random.permutation(np.resize(levels, k // 32))).repeat(32)
    a = np.empty((k // 512, 16))
    for p in range(k // 512):
        a[p, :8] = np.random.permutation(np.resize(levels, 8))
        for g in range(8):
            far = levels[np.abs(levels - a[p, g]) >= 10]
            a[p, g + 8] = far[np.random.randint(len(far))]
    return np.exp2(a.ravel()).repeat(32)


def f64(x):
    return np.asarray(x).astype(np.float64)


def sigmoid(v):
    return 1.0 / (1.0 + np.exp(-v))


G, D, M, O, N = 4, 128, 128, 128, 512


def setup_inputs():
    n = np.random.standard_normal
    s_d = mx_kscale(D, 0)
    s_o = mx_kscale(O, 0)
    return {
        "x": (n((G, D, N)) * s_d[:, None]).astype(np.float32),
        "w1": (n((G, D, M)) / np.sqrt(D) / s_d[:, None]).astype(np.float32),
        "w2": (n((G, D, M)) / np.sqrt(D) / s_d[:, None]).astype(np.float32),
        "th": (np.random.uniform(0.5, 1.5, (G, M, 1))).astype(np.float32),
        "wo": (n((G, O, M)) / np.sqrt(O) / s_o[:, None]).astype(np.float32),
        "dy": (n((G, O, N)) * s_o[:, None]).astype(np.float32),
        "old": (0.3 * n((G, M, N))).astype(np.float32),
    }


def reference(x, w1, w2, th, wo, dy, old):
    w1q = mxq(f64(w1), 1, "e4m3")
    xq = mxq(f64(x), 1, "e4m3")
    z1 = w1q.transpose(0, 2, 1) @ xq
    w2q = mxq(f64(w2), 1, "e4m3")
    z2 = w2q.transpose(0, 2, 1) @ xq
    mg = np.sqrt(np.square(z1) + np.square(z2) + 0.05)
    woq = mxq(f64(wo), 1, "e4m3")
    dyq = mxq(f64(dy), 1, "e4m3")
    c0 = woq.transpose(0, 2, 1) @ dyq
    dmg = c0 * sigmoid(mg - f64(th)) + c0 * mg * sigmoid(mg - f64(th)) * (1.0 - sigmoid(mg - f64(th)))
    dz1 = dmg * 0.5 / np.sqrt(np.square(z1) + np.square(z2) + 0.05) * z1 * 2.0
    y = dz1 + f64(old)
    return y

@@ -1,0 +1,190 @@
+from contextlib import ExitStack
+
+import concourse.mybir as mybir
+
+G, D, M, N = 4, 128, 128, 512
+
+F32 = mybir.dt.float32
+BF16 = mybir.dt.bfloat16
+U32 = mybir.dt.uint32
+U8 = mybir.dt.uint8
+FP8X4 = mybir.dt.float8_e4m3fn_x4
+ALU = mybir.AluOpType
+ACT = mybir.ActivationFunctionType
+
+P = 128
+PACK = 4
+ROWS = D // PACK
+N_CALL = 128
+HALF = N // 2
+
+FLOPS = 3 * 2 * G * D * M * N
+
+
+def tile_rows_bmagnitude_kernel(tc, x, w1, w2, th, wo, dy, old, out):
+    nc = tc.nc
+
+    with ExitStack() as ctx:
+        sb = ctx.enter_context(tc.tile_pool(name="sb", bufs=1))
+        ps = ctx.enter_context(tc.psum_pool(name="ps", bufs=1))
+        ctx.enter_context(tc.manual_schedule())
+
+        def load_packed(name, src):
+            width = src.shape[2]
+            raw = sb.tile([P, PACK, width], F32, name=name + "_raw")
+            nc.sync.dma_start(out=raw[:], in_=src.rearrange("g (p j) n -> (g p) j n", j=PACK))
+            return raw
+
+        def interleave(name, copy, raw):
+            width = raw.shape[2]
+            grouped = sb.tile([P, width, PACK], BF16, name=name + "_bf16", align_bytes=64)
+            copy(
+                out=grouped[:].rearrange("p (c i) j -> p c j i", i=4),
+                in_=raw[:].rearrange("p j (c i) -> p c j i", i=4),
+            )
+            return grouped
+
+        def quantize(name, grouped):
+            width = grouped.shape[1]
+            codes = sb.tile([P, width], U32, name=name + "_codes", align_bytes=64)
+            scales = sb.tile([P, width], U8, name=name + "_scales", align_bytes=64)
+            nc.vector.quantize_mx(
+                out=codes[:].bitcast(FP8X4),
+                scales=scales[:],
+                in_=grouped[:].rearrange("p n j -> p (n j)"),
+            )
+            return codes, scales
+
+        def product(banks, first_col, weights, moving):
+            w_codes, w_scales = weights
+            m_codes, m_scales = moving
+            for g in range(G):
+                rows = slice(ROWS * g, ROWS * (g + 1))
+                for c in range(0, m_codes.shape[1], N_CALL):
+                    nc.tensor.matmul_mx(
+                        out=banks[g][:, first_col + c : first_col + c + N_CALL],
+                        lhsT=w_codes[rows, :].bitcast(FP8X4),
+                        lhsT_scale=w_scales[rows, :],
+                        rhs=m_codes[rows, c : c + N_CALL].bitcast(FP8X4),
+                        rhs_scale=m_scales[rows, c : c + N_CALL],
+                        start=True,
+                        stop=True,
+                    )
+
+        halves = [slice(0, HALF), slice(HALF, N)]
+
+        xa_raw = load_packed("xa", x[:, :, halves[0]])
+        w2_raw = load_packed("w2", w2)
+        w1_raw = load_packed("w1", w1)
+        xb_raw = load_packed("xb", x[:, :, halves[1]])
+        wo_raw = load_packed("wo", wo)
+        dy_raw = load_packed("dy", dy)
+        th_sb = sb.tile([P, G], F32, name="th_sb")
+        with nc.allow_non_contiguous_dma(reason="one threshold to a partition and group"):
+            nc.sync.dma_start(out=th_sb[:], in_=th.rearrange("g m o -> m (g o)"))
+        old_sb = sb.tile([P, G, N], F32, name="old_sb")
+        nc.sync.dma_start(out=old_sb[:], in_=old.rearrange("g m n -> m g n"))
+
+        floor_src = sb.tile([P, 1], F32, name="floor_src")
+        floor = sb.tile([P, 1], F32, name="floor")
+        nc.gpsimd.memset(floor_src[:], 400.0)
+        nc.scalar.activation(out=floor[:], in_=floor_src[:], func=ACT.Abs_reciprocal_sqrt)
+
+        z1 = [ps.tile([P, N], F32, name="z1_%d" % g) for g in range(G)]
+        z2c0 = [ps.tile([P, N], F32, name="z2c0_%d" % g) for g in range(G)]
+
+        def half_tiles(name):
+            return [sb.tile([P, G, HALF], F32, name="%s_%d" % (name, h)) for h in range(2)]
+
+        def group_tiles(name):
+            return [sb.tile([P, N], F32, name="%s_%d" % (name, g)) for g in range(G)]
+
+        sq1, sq2, ssum = half_tiles("sq1"), half_tiles("sq2"), half_tiles("ssum")
+        inv = sb.tile([P, G, N], F32, name="inv")
+        mag = sb.tile([P, G, N], F32, name="mag")
+        nu, q, u, w, hh, res = (group_tiles(name) for name in ("nu", "q", "u", "w", "hh", "res"))
+
+        def square(dst, banks, h, groups):
+            for g in groups:
+                nc.scalar.activation(out=dst[h][:, g, :], in_=banks[g][:, halves[h]], func=ACT.Square)
+
+        def add_squares(h, gs):
+            nc.vector.scalar_tensor_tensor(
+                out=ssum[h][:, gs, :], in0=sq2[h][:, gs, :], scalar=floor[:, 0:1], in1=sq1[h][:, gs, :],
+                op0=ALU.add, op1=ALU.add,
+            )
+
+        def inverse_root(h):
+            nc.scalar.activation(out=inv[:, :, halves[h]], in_=ssum[h][:], func=ACT.Abs_reciprocal_sqrt)
+
+        def magnitude(h):
+            nc.vector.tensor_tensor(out=mag[:, :, halves[h]], in0=ssum[h][:], in1=inv[:, :, halves[h]], op=ALU.mult)
+
+        xa_bf = interleave("xa", nc.vector.tensor_copy, xa_raw)
+        w2_bf = interleave("w2", nc.scalar.copy, w2_raw)
+        w1_bf = interleave("w1", nc.scalar.copy, w1_raw)
+        xa_q = quantize("xa", xa_bf)
+        w2_q = quantize("w2", w2_bf)
+        product(z2c0, 0, w2_q, xa_q)
+        w1_q = quantize("w1", w1_bf)
+        product(z1, 0, w1_q, xa_q)
+        square(sq2, z2c0, 0, range(G))
+        square(sq1, z1, 0, range(G))
+
+        xb_bf = interleave("xb", nc.vector.tensor_copy, xb_raw)
+        wo_bf = interleave("wo", nc.vector.tensor_copy, wo_raw)
+        xb_q = quantize("xb", xb_bf)
+        wo_q = quantize("wo", wo_bf)
+        product(z2c0, HALF, w2_q, xb_q)
+        product(z1, HALF, w1_q, xb_q)
+        add_squares(0, slice(0, G))
+        for g in range(G):
+            square(sq2, z2c0, 1, [g])
+            square(sq1, z1, 1, [g])
+        dy_bf = interleave("dy", nc.vector.tensor_copy, dy_raw)
+        add_squares(1, slice(0, 2))
+        add_squares(1, slice(2, G))
+        inverse_root(0)
+        inverse_root(1)
+        dy_q = quantize("dy", dy_bf)
+        product(z2c0, 0, wo_q, dy_q)
+        magnitude(0)
+        magnitude(1)
+
+        for g in range(G):
+            nc.scalar.activation(out=nu[g][:], in_=mag[:, g, :], func=ACT.Sigmoid, bias=th_sb[:, g : g + 1], scale=-1.0)
+
+        def slope_sum(g):
+            nc.vector.tensor_tensor(out=q[g][:], in0=inv[:, g, :], in1=nu[g][:], op=ALU.add)
+
+        def times_z1(g):
+            nc.vector.scalar_tensor_tensor(
+                out=u[g][:], in0=nu[g][:], scalar=-1.0, in1=z1[g][:], op0=ALU.add, op1=ALU.mult
+            )
+
+        def times_c0(g, cols):
+            nc.vector.tensor_tensor(out=w[g][:, cols], in0=q[g][:, cols], in1=z2c0[g][:, cols], op=ALU.mult)
+
+        def join(g, cols):
+            nc.vector.tensor_tensor(out=hh[g][:, cols], in0=u[g][:, cols], in1=w[g][:, cols], op=ALU.mult)
+
+        def finish(engine, g, cols):
+            engine.tensor_tensor(out=res[g][:, cols], in0=old_sb[:, g, cols], in1=hh[g][:, cols], op=ALU.subtract)
+            nc.sync.dma_start(out=out[g, :, cols], in_=res[g][:, cols])
+
+        whole = slice(0, N)
+        slope_sum(0)
+        for g in range(G - 1):
+            times_z1(g)
+            times_c0(g, whole)
+            slope_sum(g + 1)
+            join(g, whole)
+            finish(nc.gpsimd, g, whole)
+        last = G - 1
+        times_z1(last)
+        for cols in halves:
+            times_c0(last, cols)
+        for cols in halves:
+            join(last, cols)
+        for cols in halves:
+            finish(nc.vector, last, cols)

@@ -17,6 +17,7 @@ PACK = 4
 ROWS = D // PACK
 N_CALL = 128
 HALF = N // 2
+POOL_COLS = 384
 
 FLOPS = 3 * 2 * G * D * M * N
 
@@ -117,8 +118,10 @@ def tile_rows_bmagnitude_kernel(tc, x, w1, w2, th, wo, dy, old, out):
         def inverse_root(h):
             nc.scalar.activation(out=inv[:, :, halves[h]], in_=ssum[h][:], func=ACT.Abs_reciprocal_sqrt)
 
-        def magnitude(h):
-            nc.vector.tensor_tensor(out=mag[:, :, halves[h]], in0=ssum[h][:], in1=inv[:, :, halves[h]], op=ALU.mult)
+        def magnitude(h, gs):
+            nc.vector.tensor_tensor(
+                out=mag[:, gs, halves[h]], in0=ssum[h][:, gs, :], in1=inv[:, gs, halves[h]], op=ALU.mult
+            )
 
         xa_bf = interleave("xa", nc.vector.tensor_copy, xa_raw)
         w2_bf = interleave("w2", nc.scalar.copy, w2_raw)
@@ -146,16 +149,17 @@ def tile_rows_bmagnitude_kernel(tc, x, w1, w2, th, wo, dy, old, out):
         add_squares(1, slice(2, G))
         inverse_root(0)
         inverse_root(1)
+        magnitude(0, slice(0, G))
+        magnitude(1, slice(0, 1))
         dy_q = quantize("dy", dy_bf)
         product(z2c0, 0, wo_q, dy_q)
-        magnitude(0)
-        magnitude(1)
+        magnitude(1, slice(1, G))
 
         for g in range(G):
             nc.scalar.activation(out=nu[g][:], in_=mag[:, g, :], func=ACT.Sigmoid, bias=th_sb[:, g : g + 1], scale=-1.0)
 
-        def slope_sum(g):
-            nc.vector.tensor_tensor(out=q[g][:], in0=inv[:, g, :], in1=nu[g][:], op=ALU.add)
+        def slope_sum(engine, g, cols):
+            engine.tensor_tensor(out=q[g][:, cols], in0=inv[:, g, cols], in1=nu[g][:, cols], op=ALU.add)
 
         def times_z1(g):
             nc.vector.scalar_tensor_tensor(
@@ -170,21 +174,36 @@ def tile_rows_bmagnitude_kernel(tc, x, w1, w2, th, wo, dy, old, out):
 
         def finish(engine, g, cols):
             engine.tensor_tensor(out=res[g][:, cols], in0=old_sb[:, g, cols], in1=hh[g][:, cols], op=ALU.subtract)
-            nc.sync.dma_start(out=out[g, :, cols], in_=res[g][:, cols])
+
+        def store(queue, g, cols):
+            queue.dma_start(out=out[g, :, cols], in_=res[g][:, cols])
 
         whole = slice(0, N)
-        slope_sum(0)
-        for g in range(G - 1):
+        pool_cols, rest_cols = slice(0, POOL_COLS), slice(POOL_COLS, N)
+        last = G - 1
+
+        slope_sum(nc.vector, 0, whole)
+        slope_sum(nc.gpsimd, 1, pool_cols)
+        times_z1(0)
+        times_c0(0, whole)
+        slope_sum(nc.vector, 1, rest_cols)
+        join(0, whole)
+        for g in range(1, last):
+            finish(nc.gpsimd, g - 1, pool_cols)
             times_z1(g)
             times_c0(g, whole)
-            slope_sum(g + 1)
+            finish(nc.vector, g - 1, rest_cols)
+            store(nc.sync, g - 1, whole)
+            slope_sum(nc.vector, g + 1, whole)
             join(g, whole)
-            finish(nc.gpsimd, g, whole)
-        last = G - 1
+        finish(nc.gpsimd, last - 1, pool_cols)
         times_z1(last)
         for cols in halves:
             times_c0(last, cols)
+        finish(nc.vector, last - 1, rest_cols)
+        store(nc.sync, last - 1, whole)
         for cols in halves:
             join(last, cols)
-        for cols in halves:
+        for cols, queue in zip(halves, (nc.sync, nc.scalar)):
             finish(nc.vector, last, cols)
+            store(queue, last, cols)

@@ -36,13 +36,18 @@ def tile_rows_bmagnitude_kernel(tc, x, w1, w2, th, wo, dy, old, out):
             nc.sync.dma_start(out=raw[:], in_=src.rearrange("g (p j) n -> (g p) j n", j=PACK))
             return raw
 
-        def interleave(name, copy, raw):
-            width = raw.shape[2]
-            grouped = sb.tile([P, width, PACK], BF16, name=name + "_bf16", align_bytes=64)
-            copy(
-                out=grouped[:].rearrange("p (c i) j -> p c j i", i=4),
-                in_=raw[:].rearrange("p j (c i) -> p c j i", i=4),
+        def interleave_cols(grouped, raw, cols):
+            nc.vector.tensor_copy(
+                out=grouped[:, cols, :].rearrange("p (c i) j -> p c j i", i=4),
+                in_=raw[:, :, cols].rearrange("p j (c i) -> p c j i", i=4),
             )
+
+        def bf16_tile(name, raw):
+            return sb.tile([P, raw.shape[2], PACK], BF16, name=name + "_bf16", align_bytes=64)
+
+        def interleave(name, raw):
+            grouped = bf16_tile(name, raw)
+            interleave_cols(grouped, raw, slice(0, raw.shape[2]))
             return grouped
 
         def quantize(name, grouped):
@@ -56,10 +61,10 @@ def tile_rows_bmagnitude_kernel(tc, x, w1, w2, th, wo, dy, old, out):
             )
             return codes, scales
 
-        def product(banks, first_col, weights, moving):
+        def product(banks, first_col, weights, moving, groups):
             w_codes, w_scales = weights
             m_codes, m_scales = moving
-            for g in range(G):
+            for g in groups:
                 rows = slice(ROWS * g, ROWS * (g + 1))
                 for c in range(0, m_codes.shape[1], N_CALL):
                     nc.tensor.matmul_mx(
@@ -123,36 +128,41 @@ def tile_rows_bmagnitude_kernel(tc, x, w1, w2, th, wo, dy, old, out):
                 out=mag[:, gs, halves[h]], in0=ssum[h][:, gs, :], in1=inv[:, gs, halves[h]], op=ALU.mult
             )
 
-        xa_bf = interleave("xa", nc.vector.tensor_copy, xa_raw)
-        w2_bf = interleave("w2", nc.scalar.copy, w2_raw)
-        w1_bf = interleave("w1", nc.scalar.copy, w1_raw)
+        xa_bf = interleave("xa", xa_raw)
+        w2_bf = interleave("w2", w2_raw)
         xa_q = quantize("xa", xa_bf)
         w2_q = quantize("w2", w2_bf)
-        product(z2c0, 0, w2_q, xa_q)
-        w1_q = quantize("w1", w1_bf)
-        product(z1, 0, w1_q, xa_q)
+        product(z2c0, 0, w2_q, xa_q, range(G))
         square(sq2, z2c0, 0, range(G))
+        w1_bf = interleave("w1", w1_raw)
+        w1_q = quantize("w1", w1_bf)
+        product(z1, 0, w1_q, xa_q, range(G))
         square(sq1, z1, 0, range(G))
 
-        xb_bf = interleave("xb", nc.vector.tensor_copy, xb_raw)
-        wo_bf = interleave("wo", nc.vector.tensor_copy, wo_raw)
+        xb_bf = interleave("xb", xb_raw)
         xb_q = quantize("xb", xb_bf)
+        wo_bf = interleave("wo", wo_raw)
         wo_q = quantize("wo", wo_bf)
-        product(z2c0, HALF, w2_q, xb_q)
-        product(z1, HALF, w1_q, xb_q)
-        add_squares(0, slice(0, G))
+        for g in range(G):
+            product(z2c0, HALF, w2_q, xb_q, [g])
+            product(z1, HALF, w1_q, xb_q, [g])
         for g in range(G):
             square(sq2, z2c0, 1, [g])
             square(sq1, z1, 1, [g])
-        dy_bf = interleave("dy", nc.vector.tensor_copy, dy_raw)
-        add_squares(1, slice(0, 2))
-        add_squares(1, slice(2, G))
+        dy_bf = bf16_tile("dy", dy_raw)
+        for h in range(2):
+            add_squares(h, slice(0, 2))
+            if h == 1:
+                interleave_cols(dy_bf, dy_raw, halves[1])
+            add_squares(h, slice(2, G))
+            if h == 0:
+                interleave_cols(dy_bf, dy_raw, halves[0])
         inverse_root(0)
         inverse_root(1)
+        dy_q = quantize("dy", dy_bf)
+        product(z2c0, 0, wo_q, dy_q, range(G))
         magnitude(0, slice(0, G))
         magnitude(1, slice(0, 1))
-        dy_q = quantize("dy", dy_bf)
-        product(z2c0, 0, wo_q, dy_q)
         magnitude(1, slice(1, G))
 
         for g in range(G):

from contextlib import ExitStack

import concourse.mybir as mybir

G, D, M, N = 4, 128, 128, 512

F32 = mybir.dt.float32
BF16 = mybir.dt.bfloat16
U32 = mybir.dt.uint32
U8 = mybir.dt.uint8
FP8X4 = mybir.dt.float8_e4m3fn_x4
ALU = mybir.AluOpType
ACT = mybir.ActivationFunctionType

P = 128
PACK = 4
ROWS = D // PACK
N_CALL = 128
HALF = N // 2
POOL_COLS = 384

FLOPS = 3 * 2 * G * D * M * N


def tile_rows_bmagnitude_kernel(tc, x, w1, w2, th, wo, dy, old, out):
    nc = tc.nc

    with ExitStack() as ctx:
        sb = ctx.enter_context(tc.tile_pool(name="sb", bufs=1))
        ps = ctx.enter_context(tc.psum_pool(name="ps", bufs=1))
        ctx.enter_context(tc.manual_schedule())

        def load_packed(name, src):
            width = src.shape[2]
            raw = sb.tile([P, PACK, width], F32, name=name + "_raw")
            nc.sync.dma_start(out=raw[:], in_=src.rearrange("g (p j) n -> (g p) j n", j=PACK))
            return raw

        def interleave_cols(grouped, raw, cols):
            nc.vector.tensor_copy(
                out=grouped[:, cols, :].rearrange("p (c i) j -> p c j i", i=4),
                in_=raw[:, :, cols].rearrange("p j (c i) -> p c j i", i=4),
            )

        def bf16_tile(name, raw):
            return sb.tile([P, raw.shape[2], PACK], BF16, name=name + "_bf16", align_bytes=64)

        def interleave(name, raw):
            grouped = bf16_tile(name, raw)
            interleave_cols(grouped, raw, slice(0, raw.shape[2]))
            return grouped

        def quantize(name, grouped):
            width = grouped.shape[1]
            codes = sb.tile([P, width], U32, name=name + "_codes", align_bytes=64)
            scales = sb.tile([P, width], U8, name=name + "_scales", align_bytes=64)
            nc.vector.quantize_mx(
                out=codes[:].bitcast(FP8X4),
                scales=scales[:],
                in_=grouped[:].rearrange("p n j -> p (n j)"),
            )
            return codes, scales

        def product(banks, first_col, weights, moving, groups):
            w_codes, w_scales = weights
            m_codes, m_scales = moving
            for g in groups:
                rows = slice(ROWS * g, ROWS * (g + 1))
                for c in range(0, m_codes.shape[1], N_CALL):
                    nc.tensor.matmul_mx(
                        out=banks[g][:, first_col + c : first_col + c + N_CALL],
                        lhsT=w_codes[rows, :].bitcast(FP8X4),
                        lhsT_scale=w_scales[rows, :],
                        rhs=m_codes[rows, c : c + N_CALL].bitcast(FP8X4),
                        rhs_scale=m_scales[rows, c : c + N_CALL],
                        start=True,
                        stop=True,
                    )

        halves = [slice(0, HALF), slice(HALF, N)]

        xa_raw = load_packed("xa", x[:, :, halves[0]])
        w2_raw = load_packed("w2", w2)
        w1_raw = load_packed("w1", w1)
        xb_raw = load_packed("xb", x[:, :, halves[1]])
        wo_raw = load_packed("wo", wo)
        dy_raw = load_packed("dy", dy)
        th_sb = sb.tile([P, G], F32, name="th_sb")
        with nc.allow_non_contiguous_dma(reason="one threshold to a partition and group"):
            nc.sync.dma_start(out=th_sb[:], in_=th.rearrange("g m o -> m (g o)"))
        old_sb = sb.tile([P, G, N], F32, name="old_sb")
        nc.sync.dma_start(out=old_sb[:], in_=old.rearrange("g m n -> m g n"))

        floor_src = sb.tile([P, 1], F32, name="floor_src")
        floor = sb.tile([P, 1], F32, name="floor")
        nc.gpsimd.memset(floor_src[:], 400.0)
        nc.scalar.activation(out=floor[:], in_=floor_src[:], func=ACT.Abs_reciprocal_sqrt)

        z1 = [ps.tile([P, N], F32, name="z1_%d" % g) for g in range(G)]
        z2c0 = [ps.tile([P, N], F32, name="z2c0_%d" % g) for g in range(G)]

        def half_tiles(name):
            return [sb.tile([P, G, HALF], F32, name="%s_%d" % (name, h)) for h in range(2)]

        def group_tiles(name):
            return [sb.tile([P, N], F32, name="%s_%d" % (name, g)) for g in range(G)]

        sq1, sq2, ssum = half_tiles("sq1"), half_tiles("sq2"), half_tiles("ssum")
        inv = sb.tile([P, G, N], F32, name="inv")
        mag = sb.tile([P, G, N], F32, name="mag")
        nu, q, u, w, hh, res = (group_tiles(name) for name in ("nu", "q", "u", "w", "hh", "res"))

        def square(dst, banks, h, groups):
            for g in groups:
                nc.scalar.activation(out=dst[h][:, g, :], in_=banks[g][:, halves[h]], func=ACT.Square)

        def add_squares(h, gs):
            nc.vector.scalar_tensor_tensor(
                out=ssum[h][:, gs, :], in0=sq2[h][:, gs, :], scalar=floor[:, 0:1], in1=sq1[h][:, gs, :],
                op0=ALU.add, op1=ALU.add,
            )

        def inverse_root(h):
            nc.scalar.activation(out=inv[:, :, halves[h]], in_=ssum[h][:], func=ACT.Abs_reciprocal_sqrt)

        def magnitude(h, gs):
            nc.vector.tensor_tensor(
                out=mag[:, gs, halves[h]], in0=ssum[h][:, gs, :], in1=inv[:, gs, halves[h]], op=ALU.mult
            )

        xa_bf = interleave("xa", xa_raw)
        w2_bf = interleave("w2", w2_raw)
        xa_q = quantize("xa", xa_bf)
        w2_q = quantize("w2", w2_bf)
        product(z2c0, 0, w2_q, xa_q, range(G))
        square(sq2, z2c0, 0, range(G))
        w1_bf = interleave("w1", w1_raw)
        w1_q = quantize("w1", w1_bf)
        product(z1, 0, w1_q, xa_q, range(G))
        square(sq1, z1, 0, range(G))

        xb_bf = interleave("xb", xb_raw)
        xb_q = quantize("xb", xb_bf)
        wo_bf = interleave("wo", wo_raw)
        wo_q = quantize("wo", wo_bf)
        for g in range(G):
            product(z2c0, HALF, w2_q, xb_q, [g])
            product(z1, HALF, w1_q, xb_q, [g])
        for g in range(G):
            square(sq2, z2c0, 1, [g])
            square(sq1, z1, 1, [g])
        dy_bf = bf16_tile("dy", dy_raw)
        for h in range(2):
            add_squares(h, slice(0, 2))
            if h == 1:
                interleave_cols(dy_bf, dy_raw, halves[1])
            add_squares(h, slice(2, G))
            if h == 0:
                interleave_cols(dy_bf, dy_raw, halves[0])
        inverse_root(0)
        inverse_root(1)
        dy_q = quantize("dy", dy_bf)
        product(z2c0, 0, wo_q, dy_q, range(G))
        magnitude(0, slice(0, G))
        magnitude(1, slice(0, 1))
        magnitude(1, slice(1, G))

        for g in range(G):
            nc.scalar.activation(out=nu[g][:], in_=mag[:, g, :], func=ACT.Sigmoid, bias=th_sb[:, g : g + 1], scale=-1.0)

        def slope_sum(engine, g, cols):
            engine.tensor_tensor(out=q[g][:, cols], in0=inv[:, g, cols], in1=nu[g][:, cols], op=ALU.add)

        def times_z1(g):
            nc.vector.scalar_tensor_tensor(
                out=u[g][:], in0=nu[g][:], scalar=-1.0, in1=z1[g][:], op0=ALU.add, op1=ALU.mult
            )

        def times_c0(g, cols):
            nc.vector.tensor_tensor(out=w[g][:, cols], in0=q[g][:, cols], in1=z2c0[g][:, cols], op=ALU.mult)

        def join(g, cols):
            nc.vector.tensor_tensor(out=hh[g][:, cols], in0=u[g][:, cols], in1=w[g][:, cols], op=ALU.mult)

        def finish(engine, g, cols):
            engine.tensor_tensor(out=res[g][:, cols], in0=old_sb[:, g, cols], in1=hh[g][:, cols], op=ALU.subtract)

        def store(queue, g, cols):
            queue.dma_start(out=out[g, :, cols], in_=res[g][:, cols])

        whole = slice(0, N)
        pool_cols, rest_cols = slice(0, POOL_COLS), slice(POOL_COLS, N)
        last = G - 1

        slope_sum(nc.vector, 0, whole)
        slope_sum(nc.gpsimd, 1, pool_cols)
        times_z1(0)
        times_c0(0, whole)
        slope_sum(nc.vector, 1, rest_cols)
        join(0, whole)
        for g in range(1, last):
            finish(nc.gpsimd, g - 1, pool_cols)
            times_z1(g)
            times_c0(g, whole)
            finish(nc.vector, g - 1, rest_cols)
            store(nc.sync, g - 1, whole)
            slope_sum(nc.vector, g + 1, whole)
            join(g, whole)
        finish(nc.gpsimd, last - 1, pool_cols)
        times_z1(last)
        for cols in halves:
            times_c0(last, cols)
        finish(nc.vector, last - 1, rest_cols)
        store(nc.sync, last - 1, whole)
        for cols in halves:
            join(last, cols)
        for cols, queue in zip(halves, (nc.sync, nc.scalar)):
            finish(nc.vector, last, cols)
            store(queue, last, cols)
